import numpy as np
import ml_dtypes


def mxq(x, axis, fmt="e4m3"):
    dtype, down = {"e4m3": (ml_dtypes.float8_e4m3fn, 7), "e5m2": (ml_dtypes.float8_e5m2, 14)}[fmt]
    v = np.moveaxis(np.asarray(x, np.float32).astype(ml_dtypes.bfloat16).astype(np.float64), axis, -1)
    blocks = v.reshape(v.shape[:-1] + (-1, 32))
    amax = np.abs(blocks).max(-1, keepdims=True)
    byte = np.maximum(np.where(amax > 0, np.frexp(amax)[1] - 1 + 127, 0) - down, 1)
    scale = np.exp2(byte - 127.0)
    codes = (blocks / scale).astype(np.float32).astype(dtype).astype(np.float64)
    return np.moveaxis((codes * scale).reshape(v.shape), -1, axis)


WIDE = False


def mx_kscale(k):
    if not WIDE:
        return np.ones(k)
    levels = np.array([10, -10, 5, -5, 0])
    if k % 512:
        return np.exp2(np.random.permutation(np.resize(levels, k // 32))).repeat(32)
    a = np.empty((k // 512, 16))
    for p in range(k // 512):
        a[p, :8] = np.random.permutation(np.resize(levels, 8))
        for g in range(8):
            far = levels[np.abs(levels - a[p, g]) >= 10]
            a[p, g + 8] = far[np.random.randint(len(far))]
    return np.exp2(a.ravel()).repeat(32)


def f64(x):
    return np.asarray(x).astype(np.float64)


def striped(idx):
    return np.tile(np.asarray(idx).reshape(-1, 16).T, (8, 1)).astype(np.uint16)


def unstriped(offs):
    return offs[:16].T.reshape(-1).astype(np.int64)


E2M1 = np.array([0.0, 0.5, 1.0, 1.5, 2.0, 3.0, 4.0, 6.0, -0.0, -0.5, -1.0, -1.5, -2.0, -3.0, -4.0, -6.0])


def pack_weight(w, fmt):
    k, n = w.shape
    w = f64(np.asarray(w, np.float32).astype(ml_dtypes.bfloat16)).reshape(k // 32, 32, n)
    amax = np.abs(w).max(1)
    if fmt == "e4m3":
        byte = np.frexp(amax)[1] - 1 + 127 - 7
    else:
        mant, ex = np.frexp(amax / 6.0)
        byte = np.where(mant > 0.5, ex, ex - 1) + 127
    byte = np.clip(np.where(amax > 0, byte, 1), 1, 254)
    scaled = (w * np.exp2(127.0 - byte)[:, None, :]).reshape(k, n).astype(np.float32)
    by_word = np.ascontiguousarray(scaled.reshape(k // 512, 128, 4, n).transpose(0, 1, 3, 2))
    if fmt == "e4m3":
        words = by_word.astype(ml_dtypes.float8_e4m3fn).view(np.uint8)
    else:
        c = by_word.astype(ml_dtypes.float4_e2m1fn).view(np.uint8) & 0xF
        words = (c[..., 0::2] | (c[..., 1::2] << 4)).reshape(k // 512, 128, 2 * n)
    return np.ascontiguousarray(words), np.ascontiguousarray(byte.astype(np.uint8).reshape(k // 512, 16, n))


def unpack_weight(words, scales, fmt):
    g, _, n = scales.shape
    words = np.ascontiguousarray(words).reshape(g, 128, n, -1)
    if fmt == "e4m3":
        vals = words.view(ml_dtypes.float8_e4m3fn).astype(np.float64)
    else:
        nib = np.empty((g, 128, n, 4), np.uint8)
        nib[..., 0::2] = words & 0xF
        nib[..., 1::2] = words >> 4
        vals = E2M1[nib]
    vals = vals * np.repeat(np.exp2(scales.astype(np.float64) - 127.0), 8, axis=1)[..., None]
    return vals.transpose(0, 1, 3, 2).reshape(g * 512, n)


def bf(x):
    return np.asarray(x, np.float32).astype(ml_dtypes.bfloat16)


def planes(Y):
    r, m = Y.shape
    b = f64(bf(Y)).reshape(r // 32, 32, m)
    amax = np.abs(b).max(1)
    byte = np.clip(np.where(amax > 0, np.frexp(amax)[1] - 1 + 127 - 7, 1), 1, 254)
    codes = (b * np.exp2(127.0 - byte)[:, None, :]).reshape(r, m).astype(np.float32).astype(ml_dtypes.float8_e4m3fn).view(np.uint8)
    words = codes.reshape(r // 512, 128, 4, m).transpose(0, 1, 3, 2)
    return np.ascontiguousarray(words), np.ascontiguousarray(byte.astype(np.uint8).reshape(r // 512, 16, m))


D, E, T, I, Q, V, U = 512, 512, 2048, 512, 256, 512, 1024


def setup_inputs():
    n = np.random.standard_normal
    idx = np.random.permutation(T)[:I]
    idx2 = np.random.permutation(U)[:I]
    fd = mx_kscale(D)
    fi = mx_kscale(I)
    ti = np.ones(U)
    ti[idx2] = fi
    keysp = pack_weight(n((D, T)) / fd[:, None], "e2m1")
    return {
        "query": (n((D, Q)) * 2.0 / np.sqrt(D) * fd[:, None]).astype(np.float32),
        "keys_words": keysp[0],
        "keys_scales": keysp[1],
        "is0": (np.random.uniform(0.5, 2.0, (I, 1)) * fi[:, None]).astype(np.float32),
        "vals": (n((E, T))).astype(np.float32),
        "vals2": (n((V, U)) * 1 / np.sqrt(I) / ti).astype(np.float32),
        "old": (n((E, V)) * 1.0).astype(np.float32),
        "fade": (np.random.uniform(0.2, 0.8, (E, 1))).astype(np.float32),
        "offs": striped(idx),
        "offs2": striped(idx2),
    }


def reference(query, keys_words, keys_scales, is0, vals, vals2, old, fade, offs, offs2):
    idx = unstriped(offs)
    idx2 = unstriped(offs2)
    keysu = unpack_weight(keys_words, keys_scales, "e2m1")
    queryq = mxq(f64(query), 0, "e4m3")
    keysidxg = keysu[:, idx]
    a = queryq.T @ keysidxg
    p = np.exp(a - np.max(a, axis=1, keepdims=True))
    r = p / np.sum(p, axis=1, keepdims=True)
    rt = r.T
    im0 = np.mean(rt, axis=1, keepdims=True) * f64(is0) * 512.0
    vt1 = f64(vals)[:, idx].T
    vi0 = vt1 * im0
    vt2 = f64(vals2)[:, idx2].T
    vi0q = mxq(vi0, 0, "e4m3")
    vt2q = mxq(vt2, 0, "e4m3")
    gm = vi0q.T @ vt2q
    y = gm + f64(old) * f64(fade)
    words, scales = planes(y)
    return y, words, scales

@@ -1,0 +1,223 @@
+from contextlib import ExitStack
+
+import concourse.mybir as mybir
+from concourse.masks import make_identity
+
+D, E, T, I, Q, V, U = 512, 512, 2048, 512, 256, 512, 1024
+FLOPS = 2 * Q * I * D + 2 * E * V * I
+
+F32 = mybir.dt.float32
+BF16 = mybir.dt.bfloat16
+I32 = mybir.dt.int32
+U32 = mybir.dt.uint32
+U16 = mybir.dt.uint16
+U8 = mybir.dt.uint8
+FP8X4 = mybir.dt.float8_e4m3fn_x4
+FP4X4 = mybir.dt.float4_e2m1fn_x4
+ALU = mybir.AluOpType
+ACT = mybir.ActivationFunctionType
+AXIS = mybir.AxisListType
+
+P = 128
+PACK = 4
+BANK = 512
+GROUPS = ((0, 256), (256, 128), (384, 128))
+SCALAR_BLOCKS = (0, 1, 2)
+
+
+def tile_attend_importancegram_pl_kernel(tc, query, keys_words, keys_scales, is0, vals, vals2, old, fade, offs, offs2,
+                                          out_0, out_1, out_2):
+    nc = tc.nc
+    with ExitStack() as ctx:
+        sb = ctx.enter_context(tc.tile_pool(name="sb", bufs=1))
+        ps = ctx.enter_context(tc.psum_pool(name="ps", bufs=1))
+
+        def tile(name, shape, dtype, slot=None):
+            return sb.tile(shape, dtype, name=name, tag=slot or name, align_bytes=64)
+
+        def bank(b, name, shape):
+            return ps.tile(shape, F32, name=name, tag="bank%d" % b)
+
+        key_scale_pool = tile("key_scale_pool", [P, T], U8)
+        nc.gpsimd.memset(key_scale_pool[:].bitcast(I32), 0)
+        ident = tile("ident", [P, P], F32)
+        make_identity(nc, ident[:])
+        warm = tile("warm", [P, 8], F32)
+        warm_in = tile("warm_in", [P, 8], F32)
+        nc.vector.memset(warm_in[:], 0.0)
+        nc.scalar.activation(warm[:], warm_in[:], ACT.Exp)
+
+        slots = sb.tile([P, I // 16], U16, name="slots")
+        slots2 = sb.tile([P, I // 16], U16, name="slots2")
+        key_word_pool = tile("key_word_pool", [P, T], U16)
+        q_raw = tile("q_raw", [P, PACK, Q], F32)
+        is_col = tile("is_col", [P, PACK], F32)
+        fade_col = tile("fade_col", [P, PACK], F32)
+        v1 = [tile("v1_%d" % t, [P, T], F32) for t in range(PACK)]
+        v2 = [tile("v2_%d" % b, [P, U], F32) for b in range(4)]
+        olds = [tile("old_%d" % g, [P, PACK, w], F32) for g, (c0, w) in enumerate(GROUPS)]
+        vals_t = vals.rearrange("(m t) c -> t m c", t=PACK)
+        old_v = old.rearrange("(p t) v -> p t v", t=PACK)
+        out_v = out_0.rearrange("(p t) v -> p t v", t=PACK)
+
+        nc.sync.dma_start(slots[:], offs)
+        for qd in range(4):
+            nc.sync.dma_start(key_scale_pool[32 * qd: 32 * qd + 4, :].bitcast(I32),
+                              keys_scales[0][4 * qd: 4 * qd + 4, :].bitcast(I32))
+        nc.sync.dma_start(key_word_pool[:].bitcast(I32), keys_words[0].bitcast(I32))
+        nc.sync.dma_start(q_raw[:], query.rearrange("(p j) q -> p j q", j=PACK))
+        nc.sync.dma_start(v1[0][:], vals_t[0])
+        nc.sync.dma_start(slots2[:], offs2)
+        nc.sync.dma_start(v2[0][:], vals2[0:P, :])
+        nc.sync.dma_start(is_col[:], is0.rearrange("(p r) o -> p (r o)", r=PACK))
+        nc.sync.dma_start(v1[1][:], vals_t[1])
+        nc.sync.dma_start(v2[1][:], vals2[P:2 * P, :])
+        nc.sync.dma_start(v1[2][:], vals_t[2])
+        nc.sync.dma_start(fade_col[:], fade.rearrange("(p t) o -> p (t o)", t=PACK))
+        nc.sync.dma_start(v1[3][:], vals_t[3])
+        nc.sync.dma_start(v2[2][:], vals2[2 * P:3 * P, :])
+        nc.sync.dma_start(v2[3][:], vals2[3 * P:4 * P, :])
+        for g, (c0, w) in enumerate(GROUPS):
+            nc.sync.dma_start(olds[g][:], old_v[:, :, c0:c0 + w])
+
+        key_words = tile("key_words", [P, I], U16)
+        key_scales = tile("key_scales", [P, I], U8)
+        nc.vector.tensor_copy(key_scales[:], key_scale_pool[:].indirect(slots[:]))
+        nc.vector.tensor_copy(key_words[:], key_word_pool[:].indirect(slots[:]))
+        q_bf = tile("q_bf", [P, Q, PACK], BF16)
+        nc.scalar.copy(q_bf[:], q_raw[:].rearrange("p j q -> p q j"))
+        q_codes = tile("q_codes", [P, Q], U32)
+        q_scales = tile("q_scales", [P, Q], U8)
+        nc.vector.quantize_mx(out=q_codes[:].bitcast(FP8X4), scales=q_scales[:],
+                              in_=q_bf[:].rearrange("p q j -> p (q j)"))
+        scores = [bank(h, "scores%d" % h, [P, I]) for h in range(2)]
+        for h in (1, 0):
+            rows = slice(h * P, (h + 1) * P)
+            nc.tensor.matmul_mx(out=scores[h][:], lhsT=q_codes[:, rows].bitcast(FP8X4), lhsT_scale=q_scales[:, rows],
+                                rhs=key_words[:].bitcast(FP4X4), rhs_scale=key_scales[:], start=True, stop=True)
+        neg_max = [tile("neg_max%d" % h, [P, 1], F32) for h in range(2)]
+        row_sum = [tile("row_sum%d" % h, [P, 1], F32) for h in range(2)]
+        inv_sum = [tile("inv_sum%d" % h, [P, 1], F32) for h in range(2)]
+        expo = [tile("expo%d" % h, [P, PACK, P], F32) for h in range(2)]
+        share = [tile("share%d" % h, [P, PACK, P], F32) for h in range(2)]
+        for h in (1, 0):
+            nc.vector.tensor_reduce(neg_max[h][:], scores[h][:], AXIS.X, ALU.max, negate=True)
+        for h in (1, 0):
+            nc.scalar.activation(expo[h][:], scores[h][:].rearrange("p (s r) -> p r s", r=PACK), ACT.Exp,
+                                 bias=neg_max[h][:], accum_out=row_sum[h][:])
+        for h in (1, 0):
+            nc.vector.reciprocal(inv_sum[h][:], row_sum[h][:])
+        for h in (1, 0):
+            nc.scalar.activation(share[h][:], expo[h][:], ACT.Copy, scale=inv_sum[h][:])
+        share_t = bank(2, "share_t", [P, PACK, P])
+        for r in range(PACK):
+            for h in range(2):
+                nc.tensor.matmul(share_t[:, r, :], lhsT=share[h][:, r, :], rhs=ident[:], is_transpose=True,
+                                 start=(h == 0), stop=(h == 1))
+
+        g1 = [None] * PACK
+        g1_slot = ("neg_max1", "row_sum0", "vi_bf0", "vi_bf1")
+        v1_t = [None] * PACK
+        vi_bf = [None] * PACK
+        vi_slot = (None, None, "v1_3", None)
+        cast_slot = ("expo0", "g2_0", "g2_1")
+        vi_codes = [tile("vi_codes%d" % t, [P, P], U32) for t in range(PACK)]
+        vi_scales = [tile("vi_scales%d" % t, [P, P], U8) for t in range(PACK)]
+        vt_bf = [tile("vt_bf%d" % g, [P, w, PACK], BF16) for g, (c0, w) in enumerate(GROUPS)]
+        vt_codes = [tile("vt_codes%d" % g, [P, w], U32) for g, (c0, w) in enumerate(GROUPS)]
+        vt_scales = [None] * len(GROUPS)
+        weight = tile("weight", [P, PACK], F32)
+
+        def gather1(t):
+            g1[t] = tile("g1_%d" % t, [P, I], F32, g1_slot[t])
+            nc.vector.tensor_copy(g1[t][:], v1[t][:].indirect(slots[:]))
+            v1_t[t] = bank(3 + t, "v1_t%d" % t, [P, PACK, P])
+            for r in range(PACK):
+                nc.tensor.transpose(v1_t[t][:, r, :], g1[t][:, r:I:PACK], ident[:])
+
+        def weigh1(t):
+            vi_bf[t] = tile("vi_bf%d" % t, [P, P, PACK], BF16, vi_slot[t])
+            nc.vector.tensor_tensor(vi_bf[t][:], v1_t[t][:].rearrange("p r m -> p m r"),
+                                    weight[:].unsqueeze(1).broadcast_to([P, P, PACK]), ALU.mult)
+
+        def quant1(t):
+            nc.vector.quantize_mx(out=vi_codes[t][:].bitcast(FP8X4), scales=vi_scales[t][:],
+                                  in_=vi_bf[t][:].rearrange("p m r -> p (m r)"))
+
+        def gather2(b):
+            if b in SCALAR_BLOCKS:
+                v2_bf = tile("v2_bf%d" % b, [P, U], BF16, cast_slot[b])
+                g2 = tile("g2_%d" % b, [P, I], BF16)
+                nc.scalar.activation(v2_bf[:], v2[b][:], ACT.Copy)
+                nc.scalar.activation(g2[:], v2_bf[:].indirect(slots2[:]), ACT.Copy)
+            else:
+                g2 = tile("g2_%d" % b, [P, I], BF16, "vi_bf3")
+                nc.vector.tensor_copy(g2[:], v2[b][:].indirect(slots2[:]))
+            words = g2[:].bitcast(F32)
+            v2_t = bank(7, "v2_t%d" % b, [P, 2, P])
+            for u in range(2):
+                nc.tensor.transpose(v2_t[:, u, :], words[:, u:I // 2:2], ident[:])
+            g = max(b - 1, 0)
+            first = (b * P - GROUPS[g][0]) * 2
+            pairs = vt_bf[g][:].rearrange("p m r -> p (m r)").bitcast(F32)[:, first:first + 2 * P]
+            nc.scalar.copy(pairs.rearrange("p (m u) -> p m u", u=2), v2_t[:].rearrange("p u m -> p m u"))
+
+        def quant2(g):
+            vt_scales[g] = tile("vt_scales%d" % g, [P, GROUPS[g][1]], U8, "v1_3" if g == 0 else None)
+            nc.vector.quantize_mx(out=vt_codes[g][:].bitcast(FP8X4), scales=vt_scales[g][:],
+                                  in_=vt_bf[g][:].rearrange("p m r -> p (m r)"))
+
+        gather1(0)
+        gather2(0)
+        gather1(1)
+        col_sum = tile("col_sum", [P, PACK], F32, "v1_1")
+        nc.vector.tensor_reduce(col_sum[:], share_t[:], AXIS.X, ALU.add)
+        nc.vector.scalar_tensor_tensor(weight[:], col_sum[:], float(I) / Q, is_col[:], ALU.mult, ALU.mult)
+        weigh1(0)
+        weigh1(1)
+        quant1(0)
+        gather2(1)
+        gather1(2)
+        quant1(1)
+        gather1(3)
+        weigh1(2)
+        quant1(2)
+        quant2(0)
+        weigh1(3)
+        quant1(3)
+        gather2(2)
+        gather2(3)
+        quant2(1)
+        quant2(2)
+
+        y_codes = tile("y_codes", [P, V], U32)
+        y_scales = tile("y_scales", [P, V], U8)
+        words_out = out_1[0].rearrange("p c r -> p (c r)").bitcast(I32)
+        next_bank = 0
+        for g, (c0, w) in enumerate(GROUPS):
+            cols = slice(c0, c0 + w)
+            per_bank = BANK // w
+            y = tile("y%d" % g, [P, PACK, w], F32)
+            for t0 in range(0, PACK, per_bank):
+                acc = bank(next_bank, "acc%d_%d" % (g, t0), [P, per_bank, w])
+                next_bank = next_bank + 1
+                for t in range(t0, t0 + per_bank):
+                    nc.tensor.matmul_mx(out=acc[:, t - t0, :], lhsT=vi_codes[t][:].bitcast(FP8X4),
+                                        lhsT_scale=vi_scales[t][:], rhs=vt_codes[g][:].bitcast(FP8X4),
+                                        rhs_scale=vt_scales[g][:], start=True, stop=True)
+                for t in range(t0, t0 + per_bank):
+                    nc.vector.scalar_tensor_tensor(y[:, t, :], olds[g][:, t, :], fade_col[:, t:t + 1],
+                                                   acc[:, t - t0, :], ALU.mult, ALU.add)
+            nc.sync.dma_start(out_v[:, :, cols], y[:])
+            y_bf = tile("y_bf%d" % g, [P, w, PACK], BF16)
+            if g == len(GROUPS) - 1:
+                nc.vector.tensor_copy(y_bf[:], y[:].rearrange("p t v -> p v t"))
+            else:
+                nc.scalar.copy(y_bf[:], y[:].rearrange("p t v -> p v t"))
+            nc.vector.quantize_mx(out=y_codes[:, cols].bitcast(FP8X4), scales=y_scales[:, cols],
+                                  in_=y_bf[:].rearrange("p v t -> p (v t)"))
+            nc.sync.dma_start(words_out[:, cols], y_codes[:, cols].bitcast(I32))
+        for qd in range(4):
+            queue = nc.scalar if qd % 2 else nc.sync
+            queue.dma_start(out_2[0][4 * qd: 4 * qd + 4, :].bitcast(I32),
+                            y_scales[32 * qd: 32 * qd + 4, :].bitcast(I32))

@@ -21,7 +21,10 @@ AXIS = mybir.AxisListType
 P = 128
 PACK = 4
 BANK = 512
-GROUPS = ((0, 256), (256, 128), (384, 128))
+ACC_BANKS = (0, 4, 1, 2)
+HALF = 256
+LAST_SCALAR_COLS = 96
+GROUPS = ((0, 256), (256, 256))
 SCALAR_BLOCKS = (0, 1, 2)
 
 
@@ -66,13 +69,13 @@ def tile_attend_importancegram_pl_kernel(tc, query, keys_words, keys_scales, is0
                               keys_scales[0][4 * qd: 4 * qd + 4, :].bitcast(I32))
         nc.sync.dma_start(key_word_pool[:].bitcast(I32), keys_words[0].bitcast(I32))
         nc.sync.dma_start(q_raw[:], query.rearrange("(p j) q -> p j q", j=PACK))
-        nc.sync.dma_start(v1[0][:], vals_t[0])
-        nc.sync.dma_start(slots2[:], offs2)
         nc.sync.dma_start(v2[0][:], vals2[0:P, :])
+        nc.sync.dma_start(slots2[:], offs2)
+        nc.sync.dma_start(v1[0][:], vals_t[0])
         nc.sync.dma_start(is_col[:], is0.rearrange("(p r) o -> p (r o)", r=PACK))
         nc.sync.dma_start(v1[1][:], vals_t[1])
-        nc.sync.dma_start(v2[1][:], vals2[P:2 * P, :])
         nc.sync.dma_start(v1[2][:], vals_t[2])
+        nc.sync.dma_start(v2[1][:], vals2[P:2 * P, :])
         nc.sync.dma_start(fade_col[:], fade.rearrange("(p t) o -> p (t o)", t=PACK))
         nc.sync.dma_start(v1[3][:], vals_t[3])
         nc.sync.dma_start(v2[2][:], vals2[2 * P:3 * P, :])
@@ -91,132 +94,155 @@ def tile_attend_importancegram_pl_kernel(tc, query, keys_words, keys_scales, is0
         nc.vector.quantize_mx(out=q_codes[:].bitcast(FP8X4), scales=q_scales[:],
                               in_=q_bf[:].rearrange("p q j -> p (q j)"))
         scores = [bank(h, "scores%d" % h, [P, I]) for h in range(2)]
-        for h in (1, 0):
+        for h in range(2):
             rows = slice(h * P, (h + 1) * P)
             nc.tensor.matmul_mx(out=scores[h][:], lhsT=q_codes[:, rows].bitcast(FP8X4), lhsT_scale=q_scales[:, rows],
                                 rhs=key_words[:].bitcast(FP4X4), rhs_scale=key_scales[:], start=True, stop=True)
         neg_max = [tile("neg_max%d" % h, [P, 1], F32) for h in range(2)]
-        row_sum = [tile("row_sum%d" % h, [P, 1], F32) for h in range(2)]
-        inv_sum = [tile("inv_sum%d" % h, [P, 1], F32) for h in range(2)]
+        row_sum = tile("row_sum", [P, 2], F32)
+        inv_sum = tile("inv_sum", [P, 2], F32)
         expo = [tile("expo%d" % h, [P, PACK, P], F32) for h in range(2)]
         share = [tile("share%d" % h, [P, PACK, P], F32) for h in range(2)]
-        for h in (1, 0):
+        for h in range(2):
             nc.vector.tensor_reduce(neg_max[h][:], scores[h][:], AXIS.X, ALU.max, negate=True)
-        for h in (1, 0):
+        for h in range(2):
             nc.scalar.activation(expo[h][:], scores[h][:].rearrange("p (s r) -> p r s", r=PACK), ACT.Exp,
-                                 bias=neg_max[h][:], accum_out=row_sum[h][:])
-        for h in (1, 0):
-            nc.vector.reciprocal(inv_sum[h][:], row_sum[h][:])
-        for h in (1, 0):
-            nc.scalar.activation(share[h][:], expo[h][:], ACT.Copy, scale=inv_sum[h][:])
+                                 bias=neg_max[h][:], accum_out=row_sum[:, h:h + 1])
+        nc.vector.reciprocal(inv_sum[:], row_sum[:])
+        for h in range(2):
+            nc.scalar.activation(share[h][:], expo[h][:], ACT.Copy, scale=inv_sum[:, h:h + 1])
         share_t = bank(2, "share_t", [P, PACK, P])
         for r in range(PACK):
             for h in range(2):
                 nc.tensor.matmul(share_t[:, r, :], lhsT=share[h][:, r, :], rhs=ident[:], is_transpose=True,
                                  start=(h == 0), stop=(h == 1))
-
-        g1 = [None] * PACK
-        g1_slot = ("neg_max1", "row_sum0", "vi_bf0", "vi_bf1")
-        v1_t = [None] * PACK
-        vi_bf = [None] * PACK
-        vi_slot = (None, None, "v1_3", None)
-        cast_slot = ("expo0", "g2_0", "g2_1")
-        vi_codes = [tile("vi_codes%d" % t, [P, P], U32) for t in range(PACK)]
-        vi_scales = [tile("vi_scales%d" % t, [P, P], U8) for t in range(PACK)]
-        vt_bf = [tile("vt_bf%d" % g, [P, w, PACK], BF16) for g, (c0, w) in enumerate(GROUPS)]
-        vt_codes = [tile("vt_codes%d" % g, [P, w], U32) for g, (c0, w) in enumerate(GROUPS)]
-        vt_scales = [None] * len(GROUPS)
+        factor = tile("factor", [P, PACK], F32)
+        nc.vector.tensor_scalar(factor[:], is_col[:], float(I) / Q, None, ALU.mult)
         weight = tile("weight", [P, PACK], F32)
+        scaled = tile("scaled", [P, PACK, P], F32)
+        for r in range(PACK):
+            nc.scalar.activation(scaled[:, r, :], share_t[:, r, :], ACT.Copy, scale=factor[:, r:r + 1],
+                                 accum_out=weight[:, r:r + 1])
+
+        g1_slot = ("q_bf", "inv_sum", None, "v1_2")
+        v1_t = [None] * PACK
+        vi_parts = ((0, 2, "v1_2"), (2, 1, None), (3, 1, "v2_3"))
+        vi_bf = [None] * len(vi_parts)
+        vi_codes = [tile("vi_codes%d" % k, [P, n * P], U32) for k, (t0, n, slot) in enumerate(vi_parts)]
+        vi_scales = [tile("vi_scales%d" % k, [P, n * P], U8) for k, (t0, n, slot) in enumerate(vi_parts)]
+        cast_slot = (None, "scaled", "g2_1")
+        vt_bf = [tile("vt_bf0", [P, HALF, PACK], BF16, "expo1"), tile("vt_bf1", [P, HALF, PACK], BF16)]
+        vt_codes = [tile("vt_codes%d" % g, [P, HALF], U32) for g in range(2)]
+        vt_scales = [None] * 2
 
         def gather1(t):
-            g1[t] = tile("g1_%d" % t, [P, I], F32, g1_slot[t])
-            nc.vector.tensor_copy(g1[t][:], v1[t][:].indirect(slots[:]))
+            g1 = tile("g1_%d" % t, [P, I], F32, g1_slot[t])
+            nc.vector.tensor_copy(g1[:], v1[t][:].indirect(slots[:]))
             v1_t[t] = bank(3 + t, "v1_t%d" % t, [P, PACK, P])
             for r in range(PACK):
-                nc.tensor.transpose(v1_t[t][:, r, :], g1[t][:, r:I:PACK], ident[:])
+                nc.tensor.transpose(v1_t[t][:, r, :], g1[:, r:I:PACK], ident[:])
 
-        def weigh1(t):
-            vi_bf[t] = tile("vi_bf%d" % t, [P, P, PACK], BF16, vi_slot[t])
-            nc.vector.tensor_tensor(vi_bf[t][:], v1_t[t][:].rearrange("p r m -> p m r"),
-                                    weight[:].unsqueeze(1).broadcast_to([P, P, PACK]), ALU.mult)
+        def weigh1(k):
+            t0, n, slot = vi_parts[k]
+            vi_bf[k] = tile("vi_bf%d" % k, [P, n, P, PACK], BF16, slot)
+            for t in range(t0, t0 + n):
+                nc.vector.tensor_tensor(vi_bf[k][:, t - t0, :, :], v1_t[t][:].rearrange("p r m -> p m r"),
+                                        weight[:].unsqueeze(1).broadcast_to([P, P, PACK]), ALU.mult)
 
-        def quant1(t):
-            nc.vector.quantize_mx(out=vi_codes[t][:].bitcast(FP8X4), scales=vi_scales[t][:],
-                                  in_=vi_bf[t][:].rearrange("p m r -> p (m r)"))
+        def quant1(k):
+            nc.vector.quantize_mx(out=vi_codes[k][:].bitcast(FP8X4), scales=vi_scales[k][:],
+                                  in_=vi_bf[k][:].rearrange("p n m r -> p (n m r)"))
 
         def gather2(b):
+            g2 = tile("g2_%d" % b, [P, I], BF16)
             if b in SCALAR_BLOCKS:
                 v2_bf = tile("v2_bf%d" % b, [P, U], BF16, cast_slot[b])
-                g2 = tile("g2_%d" % b, [P, I], BF16)
                 nc.scalar.activation(v2_bf[:], v2[b][:], ACT.Copy)
                 nc.scalar.activation(g2[:], v2_bf[:].indirect(slots2[:]), ACT.Copy)
             else:
-                g2 = tile("g2_%d" % b, [P, I], BF16, "vi_bf3")
                 nc.vector.tensor_copy(g2[:], v2[b][:].indirect(slots2[:]))
             words = g2[:].bitcast(F32)
-            v2_t = bank(7, "v2_t%d" % b, [P, 2, P])
+            v2_t = bank(4 if b == 3 else 7, "v2_t%d" % b, [P, 2, P])
             for u in range(2):
                 nc.tensor.transpose(v2_t[:, u, :], words[:, u:I // 2:2], ident[:])
-            g = max(b - 1, 0)
-            first = (b * P - GROUPS[g][0]) * 2
-            pairs = vt_bf[g][:].rearrange("p m r -> p (m r)").bitcast(F32)[:, first:first + 2 * P]
+            first = (b % 2) * 2 * P
+            pairs = vt_bf[b // 2][:].rearrange("p m r -> p (m r)").bitcast(F32)[:, first:first + 2 * P]
             nc.scalar.copy(pairs.rearrange("p (m u) -> p m u", u=2), v2_t[:].rearrange("p u m -> p m u"))
 
         def quant2(g):
-            vt_scales[g] = tile("vt_scales%d" % g, [P, GROUPS[g][1]], U8, "v1_3" if g == 0 else None)
+            vt_scales[g] = tile("vt_scales%d" % g, [P, HALF], U8, "v1_3" if g == 0 else None)
             nc.vector.quantize_mx(out=vt_codes[g][:].bitcast(FP8X4), scales=vt_scales[g][:],
                                   in_=vt_bf[g][:].rearrange("p m r -> p (m r)"))
 
-        gather1(0)
         gather2(0)
+        gather1(0)
         gather1(1)
-        col_sum = tile("col_sum", [P, PACK], F32, "v1_1")
-        nc.vector.tensor_reduce(col_sum[:], share_t[:], AXIS.X, ALU.add)
-        nc.vector.scalar_tensor_tensor(weight[:], col_sum[:], float(I) / Q, is_col[:], ALU.mult, ALU.mult)
-        weigh1(0)
-        weigh1(1)
-        quant1(0)
-        gather2(1)
         gather1(2)
-        quant1(1)
+        gather2(1)
+        weigh1(0)
+        quant1(0)
+        weigh1(1)
         gather1(3)
-        weigh1(2)
-        quant1(2)
+        quant1(1)
         quant2(0)
-        weigh1(3)
-        quant1(3)
         gather2(2)
         gather2(3)
-        quant2(1)
-        quant2(2)
+        weigh1(2)
 
         y_codes = tile("y_codes", [P, V], U32)
         y_scales = tile("y_scales", [P, V], U8)
         words_out = out_1[0].rearrange("p c r -> p (c r)").bitcast(I32)
-        next_bank = 0
-        for g, (c0, w) in enumerate(GROUPS):
-            cols = slice(c0, c0 + w)
-            per_bank = BANK // w
-            y = tile("y%d" % g, [P, PACK, w], F32)
-            for t0 in range(0, PACK, per_bank):
-                acc = bank(next_bank, "acc%d_%d" % (g, t0), [P, per_bank, w])
-                next_bank = next_bank + 1
-                for t in range(t0, t0 + per_bank):
-                    nc.tensor.matmul_mx(out=acc[:, t - t0, :], lhsT=vi_codes[t][:].bitcast(FP8X4),
-                                        lhsT_scale=vi_scales[t][:], rhs=vt_codes[g][:].bitcast(FP8X4),
-                                        rhs_scale=vt_scales[g][:], start=True, stop=True)
-                for t in range(t0, t0 + per_bank):
-                    nc.vector.scalar_tensor_tensor(y[:, t, :], olds[g][:, t, :], fade_col[:, t:t + 1],
-                                                   acc[:, t - t0, :], ALU.mult, ALU.add)
-            nc.sync.dma_start(out_v[:, :, cols], y[:])
-            y_bf = tile("y_bf%d" % g, [P, w, PACK], BF16)
-            if g == len(GROUPS) - 1:
-                nc.vector.tensor_copy(y_bf[:], y[:].rearrange("p t v -> p v t"))
-            else:
-                nc.scalar.copy(y_bf[:], y[:].rearrange("p t v -> p v t"))
+        part_of = (0, 0, 1, 2)
+        y = [tile("y%d" % g, [P, PACK, HALF], F32) for g in range(2)]
+        y_bf = [tile("y_bf%d" % g, [P, HALF, PACK], BF16) for g in range(2)]
+        acc = {}
+
+        def product(g, t0):
+            acc[g, t0] = bank(ACC_BANKS[2 * g + t0 // 2], "acc%d_%d" % (g, t0), [P, 2, HALF])
+            for t in range(t0, t0 + 2):
+                k = part_of[t]
+                rows = slice((t - vi_parts[k][0]) * P, (t - vi_parts[k][0] + 1) * P)
+                nc.tensor.matmul_mx(out=acc[g, t0][:, t - t0, :], lhsT=vi_codes[k][:, rows].bitcast(FP8X4),
+                                    lhsT_scale=vi_scales[k][:, rows], rhs=vt_codes[g][:].bitcast(FP8X4),
+                                    rhs_scale=vt_scales[g][:], start=True, stop=True)
+
+        def add_old(g, t):
+            nc.vector.scalar_tensor_tensor(y[g][:, t, :], olds[g][:, t, :], fade_col[:, t:t + 1],
+                                           acc[g, t - t % 2][:, t % 2, :], ALU.mult, ALU.add)
+
+        def store_y(g):
+            nc.sync.dma_start(out_v[:, :, g * HALF:(g + 1) * HALF], y[g][:])
+
+        def round_y(g):
+            split = HALF if g == 0 else LAST_SCALAR_COLS
+            nc.scalar.copy(y_bf[g][:, 0:split, :], y[g][:, :, 0:split].rearrange("p t v -> p v t"))
+            if split < HALF:
+                nc.vector.tensor_copy(y_bf[g][:, split:HALF, :], y[g][:, :, split:HALF].rearrange("p t v -> p v t"))
+
+        def planes(g):
+            cols = slice(g * HALF, (g + 1) * HALF)
             nc.vector.quantize_mx(out=y_codes[:, cols].bitcast(FP8X4), scales=y_scales[:, cols],
-                                  in_=y_bf[:].rearrange("p v t -> p (v t)"))
+                                  in_=y_bf[g][:].rearrange("p v t -> p (v t)"))
             nc.sync.dma_start(words_out[:, cols], y_codes[:, cols].bitcast(I32))
+
+        product(0, 0)
+        add_old(0, 0)
+        quant1(2)
+        add_old(0, 1)
+        quant2(1)
+        product(0, 2)
+        product(1, 0)
+        product(1, 2)
+        for t in (2, 3):
+            add_old(0, t)
+        store_y(0)
+        round_y(0)
+        for t in range(PACK):
+            add_old(1, t)
+        store_y(1)
+        round_y(1)
+        planes(0)
+        planes(1)
         for qd in range(4):
             queue = nc.scalar if qd % 2 else nc.sync
             queue.dma_start(out_2[0][4 * qd: 4 * qd + 4, :].bitcast(I32),

from contextlib import ExitStack

import concourse.mybir as mybir
from concourse.masks import make_identity

D, E, T, I, Q, V, U = 512, 512, 2048, 512, 256, 512, 1024
FLOPS = 2 * Q * I * D + 2 * E * V * I

F32 = mybir.dt.float32
BF16 = mybir.dt.bfloat16
I32 = mybir.dt.int32
U32 = mybir.dt.uint32
U16 = mybir.dt.uint16
U8 = mybir.dt.uint8
FP8X4 = mybir.dt.float8_e4m3fn_x4
FP4X4 = mybir.dt.float4_e2m1fn_x4
ALU = mybir.AluOpType
ACT = mybir.ActivationFunctionType
AXIS = mybir.AxisListType

P = 128
PACK = 4
BANK = 512
ACC_BANKS = (0, 4, 1, 2)
HALF = 256
LAST_SCALAR_COLS = 96
GROUPS = ((0, 256), (256, 256))
SCALAR_BLOCKS = (0, 1, 2)


def tile_attend_importancegram_pl_kernel(tc, query, keys_words, keys_scales, is0, vals, vals2, old, fade, offs, offs2,
                                          out_0, out_1, out_2):
    nc = tc.nc
    with ExitStack() as ctx:
        sb = ctx.enter_context(tc.tile_pool(name="sb", bufs=1))
        ps = ctx.enter_context(tc.psum_pool(name="ps", bufs=1))

        def tile(name, shape, dtype, slot=None):
            return sb.tile(shape, dtype, name=name, tag=slot or name, align_bytes=64)

        def bank(b, name, shape):
            return ps.tile(shape, F32, name=name, tag="bank%d" % b)

        key_scale_pool = tile("key_scale_pool", [P, T], U8)
        nc.gpsimd.memset(key_scale_pool[:].bitcast(I32), 0)
        ident = tile("ident", [P, P], F32)
        make_identity(nc, ident[:])
        warm = tile("warm", [P, 8], F32)
        warm_in = tile("warm_in", [P, 8], F32)
        nc.vector.memset(warm_in[:], 0.0)
        nc.scalar.activation(warm[:], warm_in[:], ACT.Exp)

        slots = sb.tile([P, I // 16], U16, name="slots")
        slots2 = sb.tile([P, I // 16], U16, name="slots2")
        key_word_pool = tile("key_word_pool", [P, T], U16)
        q_raw = tile("q_raw", [P, PACK, Q], F32)
        is_col = tile("is_col", [P, PACK], F32)
        fade_col = tile("fade_col", [P, PACK], F32)
        v1 = [tile("v1_%d" % t, [P, T], F32) for t in range(PACK)]
        v2 = [tile("v2_%d" % b, [P, U], F32) for b in range(4)]
        olds = [tile("old_%d" % g, [P, PACK, w], F32) for g, (c0, w) in enumerate(GROUPS)]
        vals_t = vals.rearrange("(m t) c -> t m c", t=PACK)
        old_v = old.rearrange("(p t) v -> p t v", t=PACK)
        out_v = out_0.rearrange("(p t) v -> p t v", t=PACK)

        nc.sync.dma_start(slots[:], offs)
        for qd in range(4):
            nc.sync.dma_start(key_scale_pool[32 * qd: 32 * qd + 4, :].bitcast(I32),
                              keys_scales[0][4 * qd: 4 * qd + 4, :].bitcast(I32))
        nc.sync.dma_start(key_word_pool[:].bitcast(I32), keys_words[0].bitcast(I32))
        nc.sync.dma_start(q_raw[:], query.rearrange("(p j) q -> p j q", j=PACK))
        nc.sync.dma_start(v2[0][:], vals2[0:P, :])
        nc.sync.dma_start(slots2[:], offs2)
        nc.sync.dma_start(v1[0][:], vals_t[0])
        nc.sync.dma_start(is_col[:], is0.rearrange("(p r) o -> p (r o)", r=PACK))
        nc.sync.dma_start(v1[1][:], vals_t[1])
        nc.sync.dma_start(v1[2][:], vals_t[2])
        nc.sync.dma_start(v2[1][:], vals2[P:2 * P, :])
        nc.sync.dma_start(fade_col[:], fade.rearrange("(p t) o -> p (t o)", t=PACK))
        nc.sync.dma_start(v1[3][:], vals_t[3])
        nc.sync.dma_start(v2[2][:], vals2[2 * P:3 * P, :])
        nc.sync.dma_start(v2[3][:], vals2[3 * P:4 * P, :])
        for g, (c0, w) in enumerate(GROUPS):
            nc.sync.dma_start(olds[g][:], old_v[:, :, c0:c0 + w])

        key_words = tile("key_words", [P, I], U16)
        key_scales = tile("key_scales", [P, I], U8)
        nc.vector.tensor_copy(key_scales[:], key_scale_pool[:].indirect(slots[:]))
        nc.vector.tensor_copy(key_words[:], key_word_pool[:].indirect(slots[:]))
        q_bf = tile("q_bf", [P, Q, PACK], BF16)
        nc.scalar.copy(q_bf[:], q_raw[:].rearrange("p j q -> p q j"))
        q_codes = tile("q_codes", [P, Q], U32)
        q_scales = tile("q_scales", [P, Q], U8)
        nc.vector.quantize_mx(out=q_codes[:].bitcast(FP8X4), scales=q_scales[:],
                              in_=q_bf[:].rearrange("p q j -> p (q j)"))
        scores = [bank(h, "scores%d" % h, [P, I]) for h in range(2)]
        for h in range(2):
            rows = slice(h * P, (h + 1) * P)
            nc.tensor.matmul_mx(out=scores[h][:], lhsT=q_codes[:, rows].bitcast(FP8X4), lhsT_scale=q_scales[:, rows],
                                rhs=key_words[:].bitcast(FP4X4), rhs_scale=key_scales[:], start=True, stop=True)
        neg_max = [tile("neg_max%d" % h, [P, 1], F32) for h in range(2)]
        row_sum = tile("row_sum", [P, 2], F32)
        inv_sum = tile("inv_sum", [P, 2], F32)
        expo = [tile("expo%d" % h, [P, PACK, P], F32) for h in range(2)]
        share = [tile("share%d" % h, [P, PACK, P], F32) for h in range(2)]
        for h in range(2):
            nc.vector.tensor_reduce(neg_max[h][:], scores[h][:], AXIS.X, ALU.max, negate=True)
        for h in range(2):
            nc.scalar.activation(expo[h][:], scores[h][:].rearrange("p (s r) -> p r s", r=PACK), ACT.Exp,
                                 bias=neg_max[h][:], accum_out=row_sum[:, h:h + 1])
        nc.vector.reciprocal(inv_sum[:], row_sum[:])
        for h in range(2):
            nc.scalar.activation(share[h][:], expo[h][:], ACT.Copy, scale=inv_sum[:, h:h + 1])
        share_t = bank(2, "share_t", [P, PACK, P])
        for r in range(PACK):
            for h in range(2):
                nc.tensor.matmul(share_t[:, r, :], lhsT=share[h][:, r, :], rhs=ident[:], is_transpose=True,
                                 start=(h == 0), stop=(h == 1))
        factor = tile("factor", [P, PACK], F32)
        nc.vector.tensor_scalar(factor[:], is_col[:], float(I) / Q, None, ALU.mult)
        weight = tile("weight", [P, PACK], F32)
        scaled = tile("scaled", [P, PACK, P], F32)
        for r in range(PACK):
            nc.scalar.activation(scaled[:, r, :], share_t[:, r, :], ACT.Copy, scale=factor[:, r:r + 1],
                                 accum_out=weight[:, r:r + 1])

        g1_slot = ("q_bf", "inv_sum", None, "v1_2")
        v1_t = [None] * PACK
        vi_parts = ((0, 2, "v1_2"), (2, 1, None), (3, 1, "v2_3"))
        vi_bf = [None] * len(vi_parts)
        vi_codes = [tile("vi_codes%d" % k, [P, n * P], U32) for k, (t0, n, slot) in enumerate(vi_parts)]
        vi_scales = [tile("vi_scales%d" % k, [P, n * P], U8) for k, (t0, n, slot) in enumerate(vi_parts)]
        cast_slot = (None, "scaled", "g2_1")
        vt_bf = [tile("vt_bf0", [P, HALF, PACK], BF16, "expo1"), tile("vt_bf1", [P, HALF, PACK], BF16)]
        vt_codes = [tile("vt_codes%d" % g, [P, HALF], U32) for g in range(2)]
        vt_scales = [None] * 2

        def gather1(t):
            g1 = tile("g1_%d" % t, [P, I], F32, g1_slot[t])
            nc.vector.tensor_copy(g1[:], v1[t][:].indirect(slots[:]))
            v1_t[t] = bank(3 + t, "v1_t%d" % t, [P, PACK, P])
            for r in range(PACK):
                nc.tensor.transpose(v1_t[t][:, r, :], g1[:, r:I:PACK], ident[:])

        def weigh1(k):
            t0, n, slot = vi_parts[k]
            vi_bf[k] = tile("vi_bf%d" % k, [P, n, P, PACK], BF16, slot)
            for t in range(t0, t0 + n):
                nc.vector.tensor_tensor(vi_bf[k][:, t - t0, :, :], v1_t[t][:].rearrange("p r m -> p m r"),
                                        weight[:].unsqueeze(1).broadcast_to([P, P, PACK]), ALU.mult)

        def quant1(k):
            nc.vector.quantize_mx(out=vi_codes[k][:].bitcast(FP8X4), scales=vi_scales[k][:],
                                  in_=vi_bf[k][:].rearrange("p n m r -> p (n m r)"))

        def gather2(b):
            g2 = tile("g2_%d" % b, [P, I], BF16)
            if b in SCALAR_BLOCKS:
                v2_bf = tile("v2_bf%d" % b, [P, U], BF16, cast_slot[b])
                nc.scalar.activation(v2_bf[:], v2[b][:], ACT.Copy)
                nc.scalar.activation(g2[:], v2_bf[:].indirect(slots2[:]), ACT.Copy)
            else:
                nc.vector.tensor_copy(g2[:], v2[b][:].indirect(slots2[:]))
            words = g2[:].bitcast(F32)
            v2_t = bank(4 if b == 3 else 7, "v2_t%d" % b, [P, 2, P])
            for u in range(2):
                nc.tensor.transpose(v2_t[:, u, :], words[:, u:I // 2:2], ident[:])
            first = (b % 2) * 2 * P
            pairs = vt_bf[b // 2][:].rearrange("p m r -> p (m r)").bitcast(F32)[:, first:first + 2 * P]
            nc.scalar.copy(pairs.rearrange("p (m u) -> p m u", u=2), v2_t[:].rearrange("p u m -> p m u"))

        def quant2(g):
            vt_scales[g] = tile("vt_scales%d" % g, [P, HALF], U8, "v1_3" if g == 0 else None)
            nc.vector.quantize_mx(out=vt_codes[g][:].bitcast(FP8X4), scales=vt_scales[g][:],
                                  in_=vt_bf[g][:].rearrange("p m r -> p (m r)"))

        gather2(0)
        gather1(0)
        gather1(1)
        gather1(2)
        gather2(1)
        weigh1(0)
        quant1(0)
        weigh1(1)
        gather1(3)
        quant1(1)
        quant2(0)
        gather2(2)
        gather2(3)
        weigh1(2)

        y_codes = tile("y_codes", [P, V], U32)
        y_scales = tile("y_scales", [P, V], U8)
        words_out = out_1[0].rearrange("p c r -> p (c r)").bitcast(I32)
        part_of = (0, 0, 1, 2)
        y = [tile("y%d" % g, [P, PACK, HALF], F32) for g in range(2)]
        y_bf = [tile("y_bf%d" % g, [P, HALF, PACK], BF16) for g in range(2)]
        acc = {}

        def product(g, t0):
            acc[g, t0] = bank(ACC_BANKS[2 * g + t0 // 2], "acc%d_%d" % (g, t0), [P, 2, HALF])
            for t in range(t0, t0 + 2):
                k = part_of[t]
                rows = slice((t - vi_parts[k][0]) * P, (t - vi_parts[k][0] + 1) * P)
                nc.tensor.matmul_mx(out=acc[g, t0][:, t - t0, :], lhsT=vi_codes[k][:, rows].bitcast(FP8X4),
                                    lhsT_scale=vi_scales[k][:, rows], rhs=vt_codes[g][:].bitcast(FP8X4),
                                    rhs_scale=vt_scales[g][:], start=True, stop=True)

        def add_old(g, t):
            nc.vector.scalar_tensor_tensor(y[g][:, t, :], olds[g][:, t, :], fade_col[:, t:t + 1],
                                           acc[g, t - t % 2][:, t % 2, :], ALU.mult, ALU.add)

        def store_y(g):
            nc.sync.dma_start(out_v[:, :, g * HALF:(g + 1) * HALF], y[g][:])

        def round_y(g):
            split = HALF if g == 0 else LAST_SCALAR_COLS
            nc.scalar.copy(y_bf[g][:, 0:split, :], y[g][:, :, 0:split].rearrange("p t v -> p v t"))
            if split < HALF:
                nc.vector.tensor_copy(y_bf[g][:, split:HALF, :], y[g][:, :, split:HALF].rearrange("p t v -> p v t"))

        def planes(g):
            cols = slice(g * HALF, (g + 1) * HALF)
            nc.vector.quantize_mx(out=y_codes[:, cols].bitcast(FP8X4), scales=y_scales[:, cols],
                                  in_=y_bf[g][:].rearrange("p v t -> p (v t)"))
            nc.sync.dma_start(words_out[:, cols], y_codes[:, cols].bitcast(I32))

        product(0, 0)
        add_old(0, 0)
        quant1(2)
        add_old(0, 1)
        quant2(1)
        product(0, 2)
        product(1, 0)
        product(1, 2)
        for t in (2, 3):
            add_old(0, t)
        store_y(0)
        round_y(0)
        for t in range(PACK):
            add_old(1, t)
        store_y(1)
        round_y(1)
        planes(0)
        planes(1)
        for qd in range(4):
            queue = nc.scalar if qd % 2 else nc.sync
            queue.dma_start(out_2[0][4 * qd: 4 * qd + 4, :].bitcast(I32),
                            y_scales[32 * qd: 32 * qd + 4, :].bitcast(I32))
